import numpy as np
import ml_dtypes


def mxq(x, axis, fmt="e4m3"):
    dtype, down = {"e4m3": (ml_dtypes.float8_e4m3fn, 7), "e5m2": (ml_dtypes.float8_e5m2, 14)}[fmt]
    v = np.moveaxis(np.asarray(x, np.float32).astype(ml_dtypes.bfloat16).astype(np.float64), axis, -1)
    blocks = v.reshape(v.shape[:-1] + (-1, 32))
    amax = np.abs(blocks).max(-1, keepdims=True)
    byte = np.maximum(np.where(amax > 0, np.frexp(amax)[1] - 1 + 127, 0) - down, 1)
    scale = np.exp2(byte - 127.0)
    codes = (blocks / scale).astype(np.float32).astype(dtype).astype(np.float64)
    return np.moveaxis((codes * scale).reshape(v.shape), -1, axis)


WIDE = False


def mx_kscale(k):
    if not WIDE:
        return np.ones(k)
    levels = np.array([10, -10, 5, -5, 0])
    if k % 512:
        return np.exp2(np.random.permutation(np.resize(levels, k // 32))).repeat(32)
    a = np.empty((k // 512, 16))
    for p in range(k // 512):
        a[p, :8] = np.random.permutation(np.resize(levels, 8))
        for g in range(8):
            far = levels[np.abs(levels - a[p, g]) >= 10]
            a[p, g + 8] = far[np.random.randint(len(far))]
    return np.exp2(a.ravel()).repeat(32)


def f64(x):
    return np.asarray(x).astype(np.float64)


def striped8(idx):
    return np.concatenate([x.reshape(-1, 16).T for x in idx]).astype(np.uint16)


def runs(offs, k):
    lists = np.stack([offs[16 * r : 16 * r + 16].T.reshape(-1) for r in range(8)]).astype(np.int64)
    return lists[np.arange(k) % 512 // 64]


def pack_weight(w):
    k, n = w.shape
    w = f64(np.asarray(w, np.float32).astype(ml_dtypes.bfloat16)).reshape(k // 32, 32, n)
    amax = np.abs(w).max(1)
    byte = np.clip(np.where(amax > 0, np.frexp(amax)[1] - 1 + 127 - 7, 1), 1, 254)
    scaled = (w * np.exp2(127.0 - byte)[:, None, :]).reshape(k, n).astype(np.float32)
    words = np.ascontiguousarray(scaled.reshape(k // 512, 128, 4, n).transpose(0, 1, 3, 2)).astype(ml_dtypes.float8_e4m3fn).view(np.uint8)
    return words, np.ascontiguousarray(byte.astype(np.uint8).reshape(k // 512, 16, n))


def unpack_weight(words, scales):
    g, p, n, _ = words.shape
    vals = np.ascontiguousarray(words).view(ml_dtypes.float8_e4m3fn).astype(np.float64) * np.repeat(np.exp2(scales.astype(np.float64) - 127.0), 8, axis=1)[..., None]
    return vals.transpose(0, 1, 3, 2).reshape(g * 512, n)


K, T, S, N, G, H, W = 512, 1024, 512, 512, 2048, 512, 256


def setup_inputs():
    n = np.random.standard_normal
    s = mx_kscale(K)[:, None]
    u = mx_kscale(S)
    packed_xT = pack_weight(n((K, T)) * s)
    packed_dT = pack_weight(n((K, G)) / s)
    perm = np.stack([np.random.permutation(S) for _ in range(8)])
    return {
        "x_words": packed_xT[0],
        "x_scales": packed_xT[1],
        "d_words": packed_dT[0],
        "d_scales": packed_dT[1],
        "gn": (np.random.uniform(0.5, 1.5, (H, 1)) * u[:, None]).astype(np.float32),
        "w1": (n((H, N)) / np.sqrt(H) / u[:, None]).astype(np.float32),
        "offs": striped8(np.random.randint(0, T, (8, S))),
        "ka": striped8(np.random.randint(0, G, (8, H))),
        "kb": striped8(np.random.randint(0, G, (8, H))),
        "n1": striped8(perm[:, :W]),
        "n2": striped8(perm[:, W:]),
    }


def reference(x_words, x_scales, d_words, d_scales, gn, w1, offs, ka, kb, n1, n2):
    d_ka = unpack_weight(d_words, d_scales)[np.arange(K)[:, None], runs(ka, K)]
    xq = unpack_weight(x_words, x_scales)[np.arange(K)[:, None], runs(offs, K)]
    d_kb = unpack_weight(d_words, d_scales)[np.arange(K)[:, None], runs(kb, K)]
    h = 0.0625 * (d_ka.T @ xq + d_kb.T @ xq)
    z = f64(gn) * h
    h2 = mxq(f64(w1), 0, "e4m3").T @ mxq(z, 0, "e4m3")
    pb = h2[np.arange(N)[:, None], runs(n2, N)]
    pa = h2[np.arange(N)[:, None], runs(n1, N)]
    rb = pb - (0.5 * pa)
    ra = np.sqrt((pa) ** 2 + (pb) ** 2 + 0.25)
    ds = np.zeros((N, S))
    ds[np.arange(N)[:, None], runs(n1, N)] = ra
    out = ds.copy()
    out[np.arange(N)[:, None], runs(n2, N)] = rb
    return out

@@ -1,0 +1,205 @@
+from contextlib import ExitStack
+
+import concourse.mybir as mybir
+
+F32 = mybir.dt.float32
+BF16 = mybir.dt.bfloat16
+I32 = mybir.dt.int32
+U32 = mybir.dt.uint32
+U16 = mybir.dt.uint16
+U8 = mybir.dt.uint8
+FP8X4 = mybir.dt.float8_e4m3fn_x4
+ALU = mybir.AluOpType
+ACT = mybir.ActivationFunctionType
+
+P = 128
+PACK = 4
+K, T, S, N, G, H, W = 512, 1024, 512, 512, 2048, 512, 256
+CHUNK = 128
+CHUNKS = S // CHUNK
+
+FLOPS = 2 * 2 * K * H * S + 2 * H * N * S
+
+
+def tile_picked_haqipolar_none_p_kernel(
+    tc, x_words, x_scales, d_words, d_scales, gn, w1, offs, ka, kb, n1, n2, out
+):
+    nc = tc.nc
+    with ExitStack() as ctx:
+        keep = ctx.enter_context(tc.tile_pool(name="keep", bufs=1))
+        psum = ctx.enter_context(tc.psum_pool(name="psum", bufs=1))
+
+        d_bytes = keep.tile([P, G], U8, align_bytes=64)
+        x_bytes = keep.tile([P, T], U8, align_bytes=64)
+        planes = keep.tile([P, 2 * H + S], U8, align_bytes=64)
+        nc.gpsimd.memset(d_bytes[:].bitcast(I32), 0)
+        nc.vector.memset(x_bytes[:].bitcast(I32), 0)
+        nc.gpsimd.memset(planes[:].bitcast(I32), 0)
+        quarter = keep.tile([P, 1], F32)
+        nc.gpsimd.memset(quarter[:], 0.25)
+
+        ka_list = keep.tile([P, H // 16], U16)
+        kb_list = keep.tile([P, H // 16], U16)
+        x_list = keep.tile([P, S // 16], U16)
+        n1_list = keep.tile([P, W // 16], U16)
+        n2_list = keep.tile([P, W // 16], U16)
+        x_table = keep.tile([P, T], U32, align_bytes=64)
+        d_table = keep.tile([P, G], U32, align_bytes=64)
+        w_raw = [keep.tile([P, PACK, N // 2], F32, name=f"w_raw{u}", align_bytes=64) for u in range(2)]
+        gain = keep.tile([P, PACK], F32)
+
+        nc.sync.dma_start(ka_list[:], ka)
+        nc.sync.dma_start(kb_list[:], kb)
+        nc.sync.dma_start(x_list[:], offs)
+        nc.sync.dma_start(d_bytes[:].bitcast(I32)[0:P:8, :], d_scales[0].bitcast(I32))
+        nc.sync.dma_start(x_bytes[:].bitcast(I32)[0:P:8, :], x_scales[0].bitcast(I32))
+        nc.sync.dma_start(n1_list[:], n1)
+        nc.sync.dma_start(n2_list[:], n2)
+        nc.sync.dma_start(gain[:], gn.rearrange("(p t) o -> p (t o)", t=PACK))
+        nc.sync.dma_start(d_table[:].bitcast(I32), d_words[0].rearrange("p n t -> p (n t)").bitcast(I32))
+        nc.sync.dma_start(x_table[:].bitcast(I32), x_words[0].rearrange("p n t -> p (n t)").bitcast(I32))
+        w_rows = w1.rearrange("(p j) n -> p j n", j=PACK)
+        for u in range(2):
+            nc.sync.dma_start(w_raw[u][:], w_rows[:, :, u * (N // 2) : (u + 1) * (N // 2)])
+
+        d_picked_bytes = keep.tile([P, 2 * H], U8, align_bytes=64)
+        x_picked_bytes = keep.tile([P, S], U8, align_bytes=64)
+        dealt_bytes = keep.tile([P, 2 * H + S], U8, align_bytes=64)
+        nc.vector.tensor_copy(d_picked_bytes[:, 0:H], d_bytes[:].indirect(ka_list[:]))
+        nc.vector.tensor_copy(d_picked_bytes[:, H : 2 * H], d_bytes[:].indirect(kb_list[:]))
+        nc.vector.tensor_copy(x_picked_bytes[:], x_bytes[:].indirect(x_list[:]))
+        nc.vector.tensor_copy(
+            dealt_bytes[:, 0 : 2 * H].rearrange("p (a t m) -> p a m t", a=2, t=PACK),
+            d_picked_bytes[:].rearrange("p (a m t) -> p a m t", a=2, t=PACK),
+        )
+        nc.vector.tensor_copy(dealt_bytes[:, 2 * H :].bitcast(I32), x_picked_bytes[:].bitcast(I32))
+        for q in range(4):
+            nc.scalar.dma_start(
+                planes[:].bitcast(I32)[32 * q : 32 * q + 4, :],
+                dealt_bytes[:].bitcast(I32)[32 * q : 32 * q + 32 : 8, :],
+            )
+
+        x_picked = keep.tile([P, S], U32, align_bytes=64)
+        h_banks = [psum.tile([P, PACK * CHUNK], F32, name=f"h_bank{c}") for c in range(CHUNKS)]
+        d_dealt = []
+        for a, codes in enumerate((ka_list, kb_list)):
+            picked = keep.tile([P, H], U32, name=f"d_picked{a}", align_bytes=64)
+            dealt = keep.tile([P, H], U32, name=f"d_dealt{a}", align_bytes=64)
+            nc.vector.tensor_copy(picked[:], d_table[:].indirect(codes[:]))
+            if a == 0:
+                nc.vector.tensor_copy(x_picked[:], x_table[:].indirect(x_list[:]))
+            nc.vector.tensor_copy(
+                dealt[:].rearrange("p (t m) -> p m t", t=PACK),
+                picked[:].rearrange("p (m t) -> p m t", t=PACK),
+            )
+            d_dealt.append(dealt)
+
+        def first_product(a, c):
+            for t in range(PACK):
+                nc.tensor.matmul_mx(
+                    out=h_banks[c][:, t * CHUNK : (t + 1) * CHUNK],
+                    lhsT=d_dealt[a][:, t * P : (t + 1) * P].bitcast(FP8X4),
+                    lhsT_scale=planes[:, a * H + t * P : a * H + (t + 1) * P],
+                    rhs=x_picked[:, c * CHUNK : (c + 1) * CHUNK].bitcast(FP8X4),
+                    rhs_scale=planes[:, 2 * H + c * CHUNK : 2 * H + (c + 1) * CHUNK],
+                    start=(a == 0 and t == 0),
+                    stop=(a == 1 and t == PACK - 1),
+                )
+
+        for chunks in (range(CHUNKS - 1), range(CHUNKS - 1, CHUNKS)):
+            for a in range(2):
+                for c in chunks:
+                    first_product(a, c)
+
+        w_grouped = keep.tile([P, PACK * N], BF16, tag="grouped", align_bytes=64)
+        w_dealt = w_grouped[:].rearrange("p (t m j) -> p m j t", t=PACK, j=PACK)
+        for u in range(2):
+            nc.scalar.copy(
+                w_dealt[:, u * (P // 2) : (u + 1) * (P // 2)],
+                w_raw[u][:].rearrange("p j (m t) -> p m j t", t=PACK),
+            )
+        w_codes = keep.tile([P, N], U32, align_bytes=64)
+        w_plane = keep.tile([P, N], U8, align_bytes=64)
+        nc.vector.quantize_mx(out=w_codes[:].bitcast(FP8X4), scales=w_plane[:], in_=w_grouped[:])
+
+        z_all = keep.tile([P, CHUNKS * CHUNK * PACK], BF16, tag="grouped", align_bytes=64)
+        z_grouped = [z_all[:, c * CHUNK * PACK : (c + 1) * CHUNK * PACK] for c in range(CHUNKS)]
+
+        def round_z(c):
+            nc.vector.scalar_tensor_tensor(
+                out=z_grouped[c].rearrange("p (n t) -> p n t", t=PACK),
+                in0=h_banks[c][:].rearrange("p (t n) -> p n t", t=PACK),
+                scalar=0.0625,
+                in1=gain[:].unsqueeze(1).to_broadcast([P, CHUNK, PACK]),
+                op0=ALU.mult,
+                op1=ALU.mult,
+            )
+
+        h2_banks = [psum.tile([P, S], F32, name=f"h2_bank{t}") for t in range(PACK)]
+
+        def second_product(c):
+            cols = slice(c * CHUNK, (c + 1) * CHUNK)
+            z_codes = keep.tile([P, CHUNK], U32, name=f"z_codes{c}", align_bytes=64)
+            z_plane = keep.tile([P, CHUNK], U8, name=f"z_plane{c}", align_bytes=64)
+            nc.vector.quantize_mx(out=z_codes[:].bitcast(FP8X4), scales=z_plane[:], in_=z_grouped[c])
+            for t in range(PACK):
+                nc.tensor.matmul_mx(
+                    out=h2_banks[t][:, cols],
+                    lhsT=w_codes[:, t * P : (t + 1) * P].bitcast(FP8X4),
+                    lhsT_scale=w_plane[:, t * P : (t + 1) * P],
+                    rhs=z_codes[:].bitcast(FP8X4),
+                    rhs_scale=z_plane[:],
+                    start=True,
+                    stop=True,
+                )
+
+        h2 = [None] * PACK
+        for t in range(2):
+            h2[t] = keep.tile([P, S], F32, name=f"h2_{t}", tag=f"turn{t % 2}")
+        first, second = slice(0, S // 2), slice(S // 2, S)
+
+        round_z(0)
+        round_z(1)
+        second_product(0)
+        round_z(2)
+        second_product(1)
+        nc.scalar.copy(h2[0][:, first], h2_banks[0][:, first])
+        nc.scalar.copy(h2[1][:, first], h2_banks[1][:, first])
+        round_z(3)
+        second_product(2)
+        second_product(3)
+        nc.scalar.copy(h2[0][:, second], h2_banks[0][:, second])
+        nc.vector.tensor_copy(h2[1][:, second], h2_banks[1][:, second])
+
+        out_rows = out.rearrange("(p t) n -> t p n", t=PACK)
+        totals = [keep.tile([P, W], F32, name=f"total{t}") for t in range(PACK)]
+        results = [keep.tile([P, S], F32, name=f"result{t}") for t in range(PACK)]
+
+        def fetch_pairs(t):
+            if t >= 2:
+                h2[t] = keep.tile([P, S], F32, name=f"h2_{t}", tag=f"turn{t % 2}")
+                nc.scalar.copy(h2[t][:], h2_banks[t][:])
+            pair = keep.tile([P, 2 * W], F32, name=f"pair{t}")
+            nc.scalar.activation(pair[:, 0:W], h2[t][:].indirect(n1_list[:]), ACT.Copy, scale=-0.5)
+            if t == 0:
+                nc.vector.tensor_copy(pair[:, W:], h2[t][:].indirect(n2_list[:]))
+            else:
+                nc.scalar.activation(pair[:, W:], h2[t][:].indirect(n2_list[:]), ACT.Copy)
+            nc.vector.tensor_tensor(results[t][:].indirect(n2_list[:]), pair[:, 0:W], pair[:, W:], ALU.add)
+            squares = keep.tile([P, 2 * W], F32, name=f"squares{t}")
+            nc.scalar.activation(squares[:], pair[:], ACT.Square)
+            nc.vector.scalar_tensor_tensor(
+                out=totals[t][:], in0=squares[:, 0:W], scalar=4.0, in1=squares[:, W:], op0=ALU.mult, op1=ALU.add
+            )
+
+        def put_roots(t):
+            root = keep.tile([P, W], F32, name=f"root{t}", tag=f"turn{(t + 1) % 2}")
+            nc.scalar.activation(root[:], totals[t][:], ACT.Sqrt, bias=quarter[:])
+            nc.vector.tensor_copy(results[t][:].indirect(n1_list[:]), root[:])
+            nc.sync.dma_start(out_rows[t], results[t][:])
+
+        fetch_pairs(0)
+        for t in range(1, PACK):
+            fetch_pairs(t)
+            put_roots(t - 1)
+        put_roots(PACK - 1)

@@ -38,6 +38,9 @@ def tile_picked_haqipolar_none_p_kernel(
         quarter = keep.tile([P, 1], F32)
         nc.gpsimd.memset(quarter[:], 0.25)
 
+        warm = keep.tile([P, 1], F32)
+        nc.scalar.activation(warm[:], quarter[:], ACT.Sqrt)
+
         ka_list = keep.tile([P, H // 16], U16)
         kb_list = keep.tile([P, H // 16], U16)
         x_list = keep.tile([P, S // 16], U16)

@@ -32,8 +32,8 @@ def tile_picked_haqipolar_none_p_kernel(
         d_bytes = keep.tile([P, G], U8, align_bytes=64)
         x_bytes = keep.tile([P, T], U8, align_bytes=64)
         planes = keep.tile([P, 2 * H + S], U8, align_bytes=64)
-        nc.gpsimd.memset(d_bytes[:].bitcast(I32), 0)
-        nc.vector.memset(x_bytes[:].bitcast(I32), 0)
+        nc.vector.memset(d_bytes[:].bitcast(I32), 0)
+        nc.gpsimd.memset(x_bytes[:].bitcast(I32), 0)
         nc.gpsimd.memset(planes[:].bitcast(I32), 0)
         quarter = keep.tile([P, 1], F32)
         nc.gpsimd.memset(quarter[:], 0.25)
@@ -51,51 +51,49 @@ def tile_picked_haqipolar_none_p_kernel(
         w_raw = [keep.tile([P, PACK, N // 2], F32, name=f"w_raw{u}", align_bytes=64) for u in range(2)]
         gain = keep.tile([P, PACK], F32)
 
+        nc.sync.dma_start(x_list[:], offs)
         nc.sync.dma_start(ka_list[:], ka)
         nc.sync.dma_start(kb_list[:], kb)
-        nc.sync.dma_start(x_list[:], offs)
-        nc.sync.dma_start(d_bytes[:].bitcast(I32)[0:P:8, :], d_scales[0].bitcast(I32))
         nc.sync.dma_start(x_bytes[:].bitcast(I32)[0:P:8, :], x_scales[0].bitcast(I32))
+        nc.sync.dma_start(d_bytes[:].bitcast(I32)[0:P:8, :], d_scales[0].bitcast(I32))
         nc.sync.dma_start(n1_list[:], n1)
         nc.sync.dma_start(n2_list[:], n2)
-        nc.sync.dma_start(gain[:], gn.rearrange("(p t) o -> p (t o)", t=PACK))
         nc.sync.dma_start(d_table[:].bitcast(I32), d_words[0].rearrange("p n t -> p (n t)").bitcast(I32))
         nc.sync.dma_start(x_table[:].bitcast(I32), x_words[0].rearrange("p n t -> p (n t)").bitcast(I32))
         w_rows = w1.rearrange("(p j) n -> p j n", j=PACK)
         for u in range(2):
             nc.sync.dma_start(w_raw[u][:], w_rows[:, :, u * (N // 2) : (u + 1) * (N // 2)])
+        nc.sync.dma_start(gain[:], gn.rearrange("(p t) o -> p (t o)", t=PACK))
 
-        d_picked_bytes = keep.tile([P, 2 * H], U8, align_bytes=64)
+        d_picked_bytes = [keep.tile([P, H], U8, name=f"d_picked_bytes{a}", align_bytes=64) for a in range(2)]
         x_picked_bytes = keep.tile([P, S], U8, align_bytes=64)
         dealt_bytes = keep.tile([P, 2 * H + S], U8, align_bytes=64)
-        nc.vector.tensor_copy(d_picked_bytes[:, 0:H], d_bytes[:].indirect(ka_list[:]))
-        nc.vector.tensor_copy(d_picked_bytes[:, H : 2 * H], d_bytes[:].indirect(kb_list[:]))
         nc.vector.tensor_copy(x_picked_bytes[:], x_bytes[:].indirect(x_list[:]))
-        nc.vector.tensor_copy(
-            dealt_bytes[:, 0 : 2 * H].rearrange("p (a t m) -> p a m t", a=2, t=PACK),
-            d_picked_bytes[:].rearrange("p (a m t) -> p a m t", a=2, t=PACK),
-        )
+        nc.vector.tensor_copy(d_picked_bytes[0][:], d_bytes[:].indirect(ka_list[:]))
         nc.vector.tensor_copy(dealt_bytes[:, 2 * H :].bitcast(I32), x_picked_bytes[:].bitcast(I32))
+        nc.vector.tensor_copy(d_picked_bytes[1][:], d_bytes[:].indirect(kb_list[:]))
+        for a in range(2):
+            nc.vector.tensor_copy(
+                dealt_bytes[:, a * H : (a + 1) * H].rearrange("p (t m) -> p m t", t=PACK),
+                d_picked_bytes[a][:].rearrange("p (m t) -> p m t", t=PACK),
+            )
         for q in range(4):
-            nc.scalar.dma_start(
+            nc.sync.dma_start(
                 planes[:].bitcast(I32)[32 * q : 32 * q + 4, :],
                 dealt_bytes[:].bitcast(I32)[32 * q : 32 * q + 32 : 8, :],
             )
 
         x_picked = keep.tile([P, S], U32, align_bytes=64)
         h_banks = [psum.tile([P, PACK * CHUNK], F32, name=f"h_bank{c}") for c in range(CHUNKS)]
-        d_dealt = []
+        d_picked = [keep.tile([P, H], U32, name=f"d_picked{a}", align_bytes=64) for a in range(2)]
+        d_dealt = [keep.tile([P, H], U32, name=f"d_dealt{a}", align_bytes=64) for a in range(2)]
         for a, codes in enumerate((ka_list, kb_list)):
-            picked = keep.tile([P, H], U32, name=f"d_picked{a}", align_bytes=64)
-            dealt = keep.tile([P, H], U32, name=f"d_dealt{a}", align_bytes=64)
-            nc.vector.tensor_copy(picked[:], d_table[:].indirect(codes[:]))
-            if a == 0:
-                nc.vector.tensor_copy(x_picked[:], x_table[:].indirect(x_list[:]))
+            nc.vector.tensor_copy(d_picked[a][:], d_table[:].indirect(codes[:]))
+        for a in range(2):
             nc.vector.tensor_copy(
-                dealt[:].rearrange("p (t m) -> p m t", t=PACK),
-                picked[:].rearrange("p (m t) -> p m t", t=PACK),
+                d_dealt[a][:].rearrange("p (t m) -> p m t", t=PACK),
+                d_picked[a][:].rearrange("p (m t) -> p m t", t=PACK),
             )
-            d_dealt.append(dealt)
 
         def first_product(a, c):
             for t in range(PACK):
@@ -109,10 +107,13 @@ def tile_picked_haqipolar_none_p_kernel(
                     stop=(a == 1 and t == PACK - 1),
                 )
 
-        for chunks in (range(CHUNKS - 1), range(CHUNKS - 1, CHUNKS)):
+        for c in range(CHUNKS):
+            nc.vector.tensor_copy(
+                x_picked[:, c * CHUNK : (c + 1) * CHUNK],
+                x_table[:].indirect(x_list[:, c * CHUNK // 16 : (c + 1) * CHUNK // 16]),
+            )
             for a in range(2):
-                for c in chunks:
-                    first_product(a, c)
+                first_product(a, c)
 
         w_grouped = keep.tile([P, PACK * N], BF16, tag="grouped", align_bytes=64)
         w_dealt = w_grouped[:].rearrange("p (t m j) -> p m j t", t=PACK, j=PACK)

@@ -32,11 +32,11 @@ def tile_picked_haqipolar_none_p_kernel(
         d_bytes = keep.tile([P, G], U8, align_bytes=64)
         x_bytes = keep.tile([P, T], U8, align_bytes=64)
         planes = keep.tile([P, 2 * H + S], U8, align_bytes=64)
-        nc.vector.memset(d_bytes[:].bitcast(I32), 0)
         nc.gpsimd.memset(x_bytes[:].bitcast(I32), 0)
-        nc.gpsimd.memset(planes[:].bitcast(I32), 0)
+        nc.gpsimd.memset(d_bytes[:].bitcast(I32), 0)
+        nc.vector.memset(planes[:].bitcast(I32), 0)
         quarter = keep.tile([P, 1], F32)
-        nc.gpsimd.memset(quarter[:], 0.25)
+        nc.vector.memset(quarter[:], 0.25)
 
         warm = keep.tile([P, 1], F32)
         nc.scalar.activation(warm[:], quarter[:], ACT.Sqrt)
@@ -56,13 +56,13 @@ def tile_picked_haqipolar_none_p_kernel(
         nc.sync.dma_start(kb_list[:], kb)
         nc.sync.dma_start(x_bytes[:].bitcast(I32)[0:P:8, :], x_scales[0].bitcast(I32))
         nc.sync.dma_start(d_bytes[:].bitcast(I32)[0:P:8, :], d_scales[0].bitcast(I32))
-        nc.sync.dma_start(n1_list[:], n1)
-        nc.sync.dma_start(n2_list[:], n2)
         nc.sync.dma_start(d_table[:].bitcast(I32), d_words[0].rearrange("p n t -> p (n t)").bitcast(I32))
         nc.sync.dma_start(x_table[:].bitcast(I32), x_words[0].rearrange("p n t -> p (n t)").bitcast(I32))
         w_rows = w1.rearrange("(p j) n -> p j n", j=PACK)
         for u in range(2):
             nc.sync.dma_start(w_raw[u][:], w_rows[:, :, u * (N // 2) : (u + 1) * (N // 2)])
+        nc.sync.dma_start(n1_list[:], n1)
+        nc.sync.dma_start(n2_list[:], n2)
         nc.sync.dma_start(gain[:], gn.rearrange("(p t) o -> p (t o)", t=PACK))
 
         d_picked_bytes = [keep.tile([P, H], U8, name=f"d_picked_bytes{a}", align_bytes=64) for a in range(2)]

from contextlib import ExitStack

import concourse.mybir as mybir

F32 = mybir.dt.float32
BF16 = mybir.dt.bfloat16
I32 = mybir.dt.int32
U32 = mybir.dt.uint32
U16 = mybir.dt.uint16
U8 = mybir.dt.uint8
FP8X4 = mybir.dt.float8_e4m3fn_x4
ALU = mybir.AluOpType
ACT = mybir.ActivationFunctionType

P = 128
PACK = 4
K, T, S, N, G, H, W = 512, 1024, 512, 512, 2048, 512, 256
CHUNK = 128
CHUNKS = S // CHUNK

FLOPS = 2 * 2 * K * H * S + 2 * H * N * S


def tile_picked_haqipolar_none_p_kernel(
    tc, x_words, x_scales, d_words, d_scales, gn, w1, offs, ka, kb, n1, n2, out
):
    nc = tc.nc
    with ExitStack() as ctx:
        keep = ctx.enter_context(tc.tile_pool(name="keep", bufs=1))
        psum = ctx.enter_context(tc.psum_pool(name="psum", bufs=1))

        d_bytes = keep.tile([P, G], U8, align_bytes=64)
        x_bytes = keep.tile([P, T], U8, align_bytes=64)
        planes = keep.tile([P, 2 * H + S], U8, align_bytes=64)
        nc.gpsimd.memset(x_bytes[:].bitcast(I32), 0)
        nc.gpsimd.memset(d_bytes[:].bitcast(I32), 0)
        nc.vector.memset(planes[:].bitcast(I32), 0)
        quarter = keep.tile([P, 1], F32)
        nc.vector.memset(quarter[:], 0.25)

        warm = keep.tile([P, 1], F32)
        nc.scalar.activation(warm[:], quarter[:], ACT.Sqrt)

        ka_list = keep.tile([P, H // 16], U16)
        kb_list = keep.tile([P, H // 16], U16)
        x_list = keep.tile([P, S // 16], U16)
        n1_list = keep.tile([P, W // 16], U16)
        n2_list = keep.tile([P, W // 16], U16)
        x_table = keep.tile([P, T], U32, align_bytes=64)
        d_table = keep.tile([P, G], U32, align_bytes=64)
        w_raw = [keep.tile([P, PACK, N // 2], F32, name=f"w_raw{u}", align_bytes=64) for u in range(2)]
        gain = keep.tile([P, PACK], F32)

        nc.sync.dma_start(x_list[:], offs)
        nc.sync.dma_start(ka_list[:], ka)
        nc.sync.dma_start(kb_list[:], kb)
        nc.sync.dma_start(x_bytes[:].bitcast(I32)[0:P:8, :], x_scales[0].bitcast(I32))
        nc.sync.dma_start(d_bytes[:].bitcast(I32)[0:P:8, :], d_scales[0].bitcast(I32))
        nc.sync.dma_start(d_table[:].bitcast(I32), d_words[0].rearrange("p n t -> p (n t)").bitcast(I32))
        nc.sync.dma_start(x_table[:].bitcast(I32), x_words[0].rearrange("p n t -> p (n t)").bitcast(I32))
        w_rows = w1.rearrange("(p j) n -> p j n", j=PACK)
        for u in range(2):
            nc.sync.dma_start(w_raw[u][:], w_rows[:, :, u * (N // 2) : (u + 1) * (N // 2)])
        nc.sync.dma_start(n1_list[:], n1)
        nc.sync.dma_start(n2_list[:], n2)
        nc.sync.dma_start(gain[:], gn.rearrange("(p t) o -> p (t o)", t=PACK))

        d_picked_bytes = [keep.tile([P, H], U8, name=f"d_picked_bytes{a}", align_bytes=64) for a in range(2)]
        x_picked_bytes = keep.tile([P, S], U8, align_bytes=64)
        dealt_bytes = keep.tile([P, 2 * H + S], U8, align_bytes=64)
        nc.vector.tensor_copy(x_picked_bytes[:], x_bytes[:].indirect(x_list[:]))
        nc.vector.tensor_copy(d_picked_bytes[0][:], d_bytes[:].indirect(ka_list[:]))
        nc.vector.tensor_copy(dealt_bytes[:, 2 * H :].bitcast(I32), x_picked_bytes[:].bitcast(I32))
        nc.vector.tensor_copy(d_picked_bytes[1][:], d_bytes[:].indirect(kb_list[:]))
        for a in range(2):
            nc.vector.tensor_copy(
                dealt_bytes[:, a * H : (a + 1) * H].rearrange("p (t m) -> p m t", t=PACK),
                d_picked_bytes[a][:].rearrange("p (m t) -> p m t", t=PACK),
            )
        for q in range(4):
            nc.sync.dma_start(
                planes[:].bitcast(I32)[32 * q : 32 * q + 4, :],
                dealt_bytes[:].bitcast(I32)[32 * q : 32 * q + 32 : 8, :],
            )

        x_picked = keep.tile([P, S], U32, align_bytes=64)
        h_banks = [psum.tile([P, PACK * CHUNK], F32, name=f"h_bank{c}") for c in range(CHUNKS)]
        d_picked = [keep.tile([P, H], U32, name=f"d_picked{a}", align_bytes=64) for a in range(2)]
        d_dealt = [keep.tile([P, H], U32, name=f"d_dealt{a}", align_bytes=64) for a in range(2)]
        for a, codes in enumerate((ka_list, kb_list)):
            nc.vector.tensor_copy(d_picked[a][:], d_table[:].indirect(codes[:]))
        for a in range(2):
            nc.vector.tensor_copy(
                d_dealt[a][:].rearrange("p (t m) -> p m t", t=PACK),
                d_picked[a][:].rearrange("p (m t) -> p m t", t=PACK),
            )

        def first_product(a, c):
            for t in range(PACK):
                nc.tensor.matmul_mx(
                    out=h_banks[c][:, t * CHUNK : (t + 1) * CHUNK],
                    lhsT=d_dealt[a][:, t * P : (t + 1) * P].bitcast(FP8X4),
                    lhsT_scale=planes[:, a * H + t * P : a * H + (t + 1) * P],
                    rhs=x_picked[:, c * CHUNK : (c + 1) * CHUNK].bitcast(FP8X4),
                    rhs_scale=planes[:, 2 * H + c * CHUNK : 2 * H + (c + 1) * CHUNK],
                    start=(a == 0 and t == 0),
                    stop=(a == 1 and t == PACK - 1),
                )

        for c in range(CHUNKS):
            nc.vector.tensor_copy(
                x_picked[:, c * CHUNK : (c + 1) * CHUNK],
                x_table[:].indirect(x_list[:, c * CHUNK // 16 : (c + 1) * CHUNK // 16]),
            )
            for a in range(2):
                first_product(a, c)

        w_grouped = keep.tile([P, PACK * N], BF16, tag="grouped", align_bytes=64)
        w_dealt = w_grouped[:].rearrange("p (t m j) -> p m j t", t=PACK, j=PACK)
        for u in range(2):
            nc.scalar.copy(
                w_dealt[:, u * (P // 2) : (u + 1) * (P // 2)],
                w_raw[u][:].rearrange("p j (m t) -> p m j t", t=PACK),
            )
        w_codes = keep.tile([P, N], U32, align_bytes=64)
        w_plane = keep.tile([P, N], U8, align_bytes=64)
        nc.vector.quantize_mx(out=w_codes[:].bitcast(FP8X4), scales=w_plane[:], in_=w_grouped[:])

        z_all = keep.tile([P, CHUNKS * CHUNK * PACK], BF16, tag="grouped", align_bytes=64)
        z_grouped = [z_all[:, c * CHUNK * PACK : (c + 1) * CHUNK * PACK] for c in range(CHUNKS)]

        def round_z(c):
            nc.vector.scalar_tensor_tensor(
                out=z_grouped[c].rearrange("p (n t) -> p n t", t=PACK),
                in0=h_banks[c][:].rearrange("p (t n) -> p n t", t=PACK),
                scalar=0.0625,
                in1=gain[:].unsqueeze(1).to_broadcast([P, CHUNK, PACK]),
                op0=ALU.mult,
                op1=ALU.mult,
            )

        h2_banks = [psum.tile([P, S], F32, name=f"h2_bank{t}") for t in range(PACK)]

        def second_product(c):
            cols = slice(c * CHUNK, (c + 1) * CHUNK)
            z_codes = keep.tile([P, CHUNK], U32, name=f"z_codes{c}", align_bytes=64)
            z_plane = keep.tile([P, CHUNK], U8, name=f"z_plane{c}", align_bytes=64)
            nc.vector.quantize_mx(out=z_codes[:].bitcast(FP8X4), scales=z_plane[:], in_=z_grouped[c])
            for t in range(PACK):
                nc.tensor.matmul_mx(
                    out=h2_banks[t][:, cols],
                    lhsT=w_codes[:, t * P : (t + 1) * P].bitcast(FP8X4),
                    lhsT_scale=w_plane[:, t * P : (t + 1) * P],
                    rhs=z_codes[:].bitcast(FP8X4),
                    rhs_scale=z_plane[:],
                    start=True,
                    stop=True,
                )

        h2 = [None] * PACK
        for t in range(2):
            h2[t] = keep.tile([P, S], F32, name=f"h2_{t}", tag=f"turn{t % 2}")
        first, second = slice(0, S // 2), slice(S // 2, S)

        round_z(0)
        round_z(1)
        second_product(0)
        round_z(2)
        second_product(1)
        nc.scalar.copy(h2[0][:, first], h2_banks[0][:, first])
        nc.scalar.copy(h2[1][:, first], h2_banks[1][:, first])
        round_z(3)
        second_product(2)
        second_product(3)
        nc.scalar.copy(h2[0][:, second], h2_banks[0][:, second])
        nc.vector.tensor_copy(h2[1][:, second], h2_banks[1][:, second])

        out_rows = out.rearrange("(p t) n -> t p n", t=PACK)
        totals = [keep.tile([P, W], F32, name=f"total{t}") for t in range(PACK)]
        results = [keep.tile([P, S], F32, name=f"result{t}") for t in range(PACK)]

        def fetch_pairs(t):
            if t >= 2:
                h2[t] = keep.tile([P, S], F32, name=f"h2_{t}", tag=f"turn{t % 2}")
                nc.scalar.copy(h2[t][:], h2_banks[t][:])
            pair = keep.tile([P, 2 * W], F32, name=f"pair{t}")
            nc.scalar.activation(pair[:, 0:W], h2[t][:].indirect(n1_list[:]), ACT.Copy, scale=-0.5)
            if t == 0:
                nc.vector.tensor_copy(pair[:, W:], h2[t][:].indirect(n2_list[:]))
            else:
                nc.scalar.activation(pair[:, W:], h2[t][:].indirect(n2_list[:]), ACT.Copy)
            nc.vector.tensor_tensor(results[t][:].indirect(n2_list[:]), pair[:, 0:W], pair[:, W:], ALU.add)
            squares = keep.tile([P, 2 * W], F32, name=f"squares{t}")
            nc.scalar.activation(squares[:], pair[:], ACT.Square)
            nc.vector.scalar_tensor_tensor(
                out=totals[t][:], in0=squares[:, 0:W], scalar=4.0, in1=squares[:, W:], op0=ALU.mult, op1=ALU.add
            )

        def put_roots(t):
            root = keep.tile([P, W], F32, name=f"root{t}", tag=f"turn{(t + 1) % 2}")
            nc.scalar.activation(root[:], totals[t][:], ACT.Sqrt, bias=quarter[:])
            nc.vector.tensor_copy(results[t][:].indirect(n1_list[:]), root[:])
            nc.sync.dma_start(out_rows[t], results[t][:])

        fetch_pairs(0)
        for t in range(1, PACK):
            fetch_pairs(t)
            put_roots(t - 1)
        put_roots(PACK - 1)
